import numpy as np
import ml_dtypes


def mxq(x, axis, fmt="e4m3"):
    dtype, down = {"e4m3": (ml_dtypes.float8_e4m3fn, 7), "e5m2": (ml_dtypes.float8_e5m2, 14)}[fmt]
    v = np.moveaxis(np.asarray(x, np.float32).astype(ml_dtypes.bfloat16).astype(np.float64), axis, -1)
    blocks = v.reshape(v.shape[:-1] + (-1, 32))
    amax = np.abs(blocks).max(-1, keepdims=True)
    byte = np.maximum(np.where(amax > 0, np.frexp(amax)[1] - 1 + 127, 0) - down, 1)
    scale = np.exp2(byte - 127.0)
    codes = (blocks / scale).astype(np.float32).astype(dtype).astype(np.float64)
    return np.moveaxis((codes * scale).reshape(v.shape), -1, axis)


WIDE = False


def mx_kscale(k):
    if not WIDE:
        return np.ones(k)
    levels = np.array([10, -10, 5, -5, 0])
    if k % 512:
        return np.exp2(np.random.permutation(np.resize(levels, k // 32))).repeat(32)
    a = np.empty((k // 512, 16))
    for p in range(k // 512):
        a[p, :8] = np.random.permutation(np.resize(levels, 8))
        for g in range(8):
            far = levels[np.abs(levels - a[p, g]) >= 10]
            a[p, g + 8] = far[np.random.randint(len(far))]
    return np.exp2(a.ravel()).repeat(32)


def f64(x):
    return np.asarray(x).astype(np.float64)


def striped(idx):
    return np.tile(idx.reshape(-1, 16).T, (8, 1)).astype(np.uint16)


def unstriped(offs):
    return offs[:16].T.reshape(-1).astype(np.int64)


def striped8(idx):
    return np.concatenate([x.reshape(-1, 16).T for x in idx]).astype(np.uint16)


def runs(offs, k):
    lists = np.stack([offs[16 * r : 16 * r + 16].T.reshape(-1) for r in range(8)]).astype(np.int64)
    return lists[np.arange(k) % 512 // 64]


def pack_weight(w):
    k, n = w.shape
    w = f64(np.asarray(w, np.float32).astype(ml_dtypes.bfloat16)).reshape(k // 32, 32, n)
    amax = np.abs(w).max(1)
    byte = np.clip(np.where(amax > 0, np.frexp(amax)[1] - 1 + 127 - 7, 1), 1, 254)
    scaled = (w * np.exp2(127.0 - byte)[:, None, :]).reshape(k, n).astype(np.float32)
    words = np.ascontiguousarray(scaled.reshape(k // 512, 128, 4, n).transpose(0, 1, 3, 2)).astype(ml_dtypes.float8_e4m3fn).view(np.uint8)
    return words, np.ascontiguousarray(byte.astype(np.uint8).reshape(k // 512, 16, n))


def unpack_weight(words, scales):
    g, p, n, _ = words.shape
    vals = np.ascontiguousarray(words).view(ml_dtypes.float8_e4m3fn).astype(np.float64) * np.repeat(np.exp2(scales.astype(np.float64) - 127.0), 8, axis=1)[..., None]
    return vals.transpose(0, 1, 3, 2).reshape(g * 512, n)


E2M1 = np.array([0.0, 0.5, 1.0, 1.5, 2.0, 3.0, 4.0, 6.0, -0.0, -0.5, -1.0, -1.5, -2.0, -3.0, -4.0, -6.0])


def pack_fp4(w):
    k, n = w.shape
    w = f64(np.asarray(w, np.float32).astype(ml_dtypes.bfloat16)).reshape(k // 32, 32, n)
    amax = np.abs(w).max(1)
    mant, ex = np.frexp(amax / 6.0)
    byte = np.clip(np.where(amax > 0, np.where(mant > 0.5, ex, ex - 1) + 127, 1), 1, 254)
    scaled = (w * np.exp2(127.0 - byte)[:, None, :]).reshape(k, n).astype(np.float32)
    c = np.ascontiguousarray(scaled.reshape(k // 512, 128, 4, n).transpose(0, 1, 3, 2)).astype(ml_dtypes.float4_e2m1fn).view(np.uint8) & 0xF
    words = (c[..., 0::2] | (c[..., 1::2] << 4)).reshape(k // 512, 128, 2 * n)
    return np.ascontiguousarray(words), np.ascontiguousarray(byte.astype(np.uint8).reshape(k // 512, 16, n))


def unpack_fp4(words, scales):
    g, _, n = scales.shape
    words = np.ascontiguousarray(words).reshape(g, 128, n, 2)
    nib = np.empty((g, 128, n, 4), np.uint8)
    nib[..., 0::2] = words & 0xF
    nib[..., 1::2] = words >> 4
    vals = E2M1[nib] * np.repeat(np.exp2(scales.astype(np.float64) - 127.0), 8, axis=1)[..., None]
    return vals.transpose(0, 1, 3, 2).reshape(g * 512, n)


def sigmoid(v):
    return 1.0 / (1.0 + np.exp(-np.maximum(v, -700.0)))

def planes(y):
    n, m = y.shape
    v = y.astype(np.float32).astype(ml_dtypes.bfloat16).astype(np.float64).reshape(n // 32, 32, m)
    top = np.abs(v).max(1)
    byte = np.clip(np.where(top > 0, np.frexp(top)[1] - 1 + 127 - 7, 1), 1, 254)
    codes = (v * np.exp2(127.0 - byte)[:, None, :]).reshape(n, m).astype(np.float32).astype(ml_dtypes.float8_e4m3fn).view(np.uint8)
    words = codes.reshape(n // 512, 128, 4, m).transpose(0, 1, 3, 2)
    return np.ascontiguousarray(words), np.ascontiguousarray(byte.astype(np.uint8).reshape(n // 512, 16, m))


K, T, S, V, G, H = 512, 1024, 512, 512, 2048, 512


def setup_inputs():
    n = np.random.standard_normal
    s = mx_kscale(K)[:, None]
    u = mx_kscale(S)
    packed_xT = pack_weight(n((K, T)) * s)
    packed_dT = pack_weight(n((K, G)) / s)
    packed_w1 = pack_fp4(n((K, H)) / np.sqrt(K) / s)
    return {
        "x_words": packed_xT[0],
        "x_scales": packed_xT[1],
        "d_words": packed_dT[0],
        "d_scales": packed_dT[1],
        "w1_words": packed_w1[0],
        "w1_scales": packed_w1[1],
        "ga": (np.random.uniform(0.5, 1.5, (H, 1)) * u[:, None]).astype(np.float32),
        "gb": (np.random.uniform(0.5, 1.5, (H, 1)) / u[:, None]).astype(np.float32),
        "offs": striped(np.random.permutation(T)[:S]),
        "k1": striped8(np.random.randint(0, G, (8, H))),
        "two": striped(np.random.permutation(T)[:V]),
        "n1": striped(np.random.permutation(S)),
        "n2": striped(np.random.permutation(S)),
        "n3": striped8(np.stack([np.random.permutation(V) for _ in range(8)])),
        "n4": striped8(np.stack([np.random.permutation(V) for _ in range(8)])),
        "n5": striped(np.random.randint(0, V, G)),
    }


def reference(x_words, x_scales, d_words, d_scales, w1_words, w1_scales, ga, gb, offs, k1, two, n1, n2, n3, n4, n5):
    d_k1 = unpack_weight(d_words, d_scales)[np.arange(K)[:, None], runs(k1, K)]
    xq = unpack_weight(x_words, x_scales)[:, unstriped(offs)]
    a = 0.0625 * (d_k1.T @ xq)
    z = f64(ga) * (a + (sigmoid(a[:, unstriped(n1)])) * (a[:, unstriped(n2)] - a))
    x_two = unpack_weight(x_words, x_scales)[:, unstriped(two)]
    b = unpack_fp4(w1_words, w1_scales).T @ x_two
    z2 = f64(gb) * (0.75 * ((b - (b[np.arange(H)[:, None], runs(n3, H)])) * (b - (b[np.arange(H)[:, None], runs(n4, H)]))))
    s = 0.0625 * ((mxq(z, 0, "e4m3").T @ mxq(z2, 0, "e4m3")))
    mb = s[:, unstriped(n5)]
    mx = mb.reshape(S, V, 4).max(axis=2)
    mn = mb.reshape(S, V, 4).min(axis=2)
    out_0 = np.maximum(np.minimum(1.5 * s, mx), mn)
    return (out_0,) + planes(out_0)

@@ -1,0 +1,273 @@
+from contextlib import ExitStack
+
+import concourse.mybir as mybir
+
+F32 = mybir.dt.float32
+BF16 = mybir.dt.bfloat16
+I32 = mybir.dt.int32
+U32 = mybir.dt.uint32
+U16 = mybir.dt.uint16
+U8 = mybir.dt.uint8
+FP8X4 = mybir.dt.float8_e4m3fn_x4
+FP4X4 = mybir.dt.float4_e2m1fn_x4
+ALU = mybir.AluOpType
+ACT = mybir.ActivationFunctionType
+
+P = 128
+PACK = 4
+T, G, S = 1024, 2048, 512
+MEMBERS = 4
+HALF = S // 2
+S_WINDOW = 1056
+W_WINDOW = 528
+CHUNKS = (256, 128, 128)
+FLOPS = 3 * 2 * 512 * 512 * 512
+
+
+def tile_picked_ckqtrackquadgclip_none_po_kernel(
+    tc, x_words, x_scales, d_words, d_scales, w1_words, w1_scales, ga, gb, offs, k1, two, n1, n2, n3, n4, n5, out_0, out_1, out_2
+):
+    nc = tc.nc
+    with ExitStack() as ctx:
+        keep = ctx.enter_context(tc.tile_pool(name="keep", bufs=1))
+        ring = ctx.enter_context(tc.tile_pool(name="ring", bufs=3))
+        gates = ctx.enter_context(tc.tile_pool(name="gates", bufs=5))
+        psum = ctx.enter_context(tc.psum_pool(name="psum", bufs=1))
+
+        def held(name, shape, dtype):
+            return keep.tile(shape, dtype, name=name, align_bytes=64)
+
+        def load_list(name, src):
+            dst = keep.tile(list(src.shape), U16, name=name)
+            nc.sync.dma_start(dst[:], src)
+            return dst
+
+        def entries(lst, start, count):
+            return lst[:, start // 16 : (start + count) // 16]
+
+        xw = held("xw", [P, T], U32)
+        xs = held("xs", [P, T], U8)
+        dw = held("dw", [P, G], U32)
+        ds = held("ds", [P, G], U8)
+        ww = held("ww", [P, 2 * S], U8)
+        ws = held("ws", [P, S], U8)
+        nc.gpsimd.memset(ws[:].bitcast(I32), 0)
+        nc.gpsimd.memset(xs[:].bitcast(I32), 0)
+        nc.vector.memset(ds[:].bitcast(I32), 0)
+
+        two_l = load_list("two_l", two)
+        nc.sync.dma_start(xw[:].bitcast(I32), x_words[0].rearrange("p n t -> p (n t)").bitcast(I32))
+        nc.scalar.dma_start(ww[:].bitcast(I32), w1_words[0].bitcast(I32))
+        for q in range(4):
+            nc.scalar.dma_start(ws[32 * q : 32 * q + 4, :].bitcast(I32), w1_scales[0, 4 * q : 4 * q + 4, :].bitcast(I32))
+        for q, queue in enumerate((nc.gpsimd, nc.gpsimd, nc.sync, nc.sync)):
+            queue.dma_start(xs[32 * q : 32 * q + 4, :].bitcast(I32), x_scales[0, 4 * q : 4 * q + 4, :].bitcast(I32))
+        k1_l = load_list("k1_l", k1)
+        for e in range(2):
+            nc.sync.dma_start(ds[e:P:16, :].bitcast(I32), d_scales[0, e:16:2, :].bitcast(I32))
+        n3_l = load_list("n3_l", n3)
+        offs_l = load_list("offs_l", offs)
+        nc.sync.dma_start(dw[:].bitcast(I32), d_words[0].rearrange("p n t -> p (n t)").bitcast(I32))
+        n4_l = load_list("n4_l", n4)
+        gb_raw = held("gb_raw", [P, PACK], F32)
+        ga_raw = held("ga_raw", [P, PACK], F32)
+        nc.sync.dma_start(gb_raw[:], gb.rearrange("(p t) o -> p (t o)", t=PACK))
+        nc.sync.dma_start(ga_raw[:], ga.rearrange("(p t) o -> p (t o)", t=PACK))
+        n1_l = load_list("n1_l", n1)
+        n2_l = load_list("n2_l", n2)
+        n5_l = load_list("n5_l", n5)
+
+        b_wins = [held("b_win%d" % t, [P, 2 * S], F32) for t in range(PACK)]
+        a_win = [held("a_win%d" % t, [P, 2 * S], F32) for t in range(PACK)]
+        w_win = [held("w_win%d" % t, [P, W_WINDOW], F32) for t in range(PACK)]
+        s_win = [held("s_win%d" % t, [P, S_WINDOW], F32) for t in range(PACK)]
+
+        gb34 = held("gb34", [P, PACK], F32)
+        ga16 = held("ga16", [P, PACK], F32)
+        nc.gpsimd.tensor_scalar(ga16[:], ga_raw[:], 0.0625, 0.0, ALU.mult, ALU.add)
+        nc.gpsimd.tensor_scalar(gb34[:], gb_raw[:], 0.75, 0.0, ALU.mult, ALU.add)
+
+        ww_d = held("ww_d", [P, 2 * S], U8)
+        ws_d = held("ws_d", [P, S], U8)
+        nc.scalar.copy(
+            ww_d[:].bitcast(U16).rearrange("p (t m) -> p t m", t=PACK), ww[:].bitcast(U16).rearrange("p (m t) -> p t m", t=PACK)
+        )
+        nc.vector.tensor_copy(ws_d[:].rearrange("p (t m) -> p t m", t=PACK), ws[:].rearrange("p (m t) -> p t m", t=PACK))
+
+        x2w = held("x2w", [P, S], U32)
+        x2s = held("x2s", [P, S], U8)
+        nc.vector.tensor_copy(x2w[:], xw[:].indirect(two_l[:]))
+        nc.vector.tensor_copy(x2s[:], xs[:].indirect(two_l[:]))
+        dks = held("dks", [P, S], U8)
+        dks_d = held("dks_d", [P, S], U8)
+        nc.vector.tensor_copy(dks[:], ds[:].indirect(k1_l[:]))
+        nc.vector.tensor_copy(dks_d[:].rearrange("p (t m) -> p t m", t=PACK), dks[:].rearrange("p (m t) -> p t m", t=PACK))
+        for e in range(2):
+            nc.sync.dma_start(dks_d[2 + e : P : 32, :].bitcast(I32), dks_d[16 + e : P : 32, :].bitcast(I32))
+        xqw = held("xqw", [P, S], U32)
+        xqs = held("xqs", [P, S], U8)
+        nc.vector.tensor_copy(xqw[:], xw[:].indirect(offs_l[:]))
+        nc.vector.tensor_copy(xqs[:], xs[:].indirect(offs_l[:]))
+        dkw = keep.tile([P, S], U32, name="dkw", tag="first_difference", align_bytes=64)
+        dkw_d = held("dkw_d", [P, S], U32)
+        nc.vector.tensor_copy(dkw[:], dw[:].indirect(k1_l[:]))
+        nc.vector.tensor_copy(dkw_d[:].rearrange("p (t m) -> p m t", t=PACK), dkw[:].rearrange("p (m t) -> p m t", t=PACK))
+
+        z2_planes = held("z2_planes", [P, PACK, S], BF16)
+        z2_w = held("z2_w", [P, S], U32)
+        z2_s = held("z2_s", [P, S], U8)
+
+        def b_tile(t, bank):
+            acc = psum.tile([P, S], F32, name="bank%d" % bank)
+            nc.tensor.matmul_mx(
+                out=acc[:],
+                lhsT=ww_d[:, 2 * P * t : 2 * P * (t + 1)].bitcast(FP4X4),
+                lhsT_scale=ws_d[:, P * t : P * (t + 1)],
+                rhs=x2w[:].bitcast(FP8X4),
+                rhs_scale=x2s[:],
+                start=True,
+                stop=True,
+            )
+            b_win = b_wins[t]
+            nc.scalar.copy(b_win[:, :S], acc[:])
+            b34 = ring.tile([P, 2, S], F32, name="b34")
+            for which, lst in enumerate((n3_l, n4_l)):
+                nc.scalar.activation(b34[:, which, :], b_win[:].indirect(lst[:]), ACT.Copy)
+            if t == 0:
+                d34 = keep.tile([P, 2, S], F32, name="d34_first", tag="first_difference", align_bytes=64)
+            else:
+                d34 = ring.tile([P, 2, S], F32, name="d34")
+            nc.vector.tensor_tensor(d34[:], b34[:], b_win[:, :S].unsqueeze(1).to_broadcast([P, 2, S]), ALU.subtract)
+            nc.vector.scalar_tensor_tensor(z2_planes[:, t, :], d34[:, 0, :], gb34[:, t : t + 1], d34[:, 1, :], ALU.mult, ALU.mult)
+
+        def quantise_z2():
+            z2_b = held("z2_b", [P, S * PACK], BF16)
+            nc.vector.tensor_copy(
+                z2_b[:].rearrange("p (c i t) -> p c t i", i=4, t=PACK), z2_planes[:].rearrange("p t (c i) -> p c t i", i=4)
+            )
+            nc.vector.quantize_mx(out=z2_w[:].bitcast(FP8X4), scales=z2_s[:], in_=z2_b[:])
+
+        z_b = held("z_b", [P, S * PACK], BF16)
+        z_view = z_b[:].rearrange("p (i c t) -> p c t i", i=PACK, t=PACK)
+        far = held("far", [P, PACK, S], F32)
+        near = held("near", [P, PACK, S], F32)
+
+        def a_tile(t, bank):
+            acc = psum.tile([P, S], F32, name="bank%d" % bank)
+            nc.tensor.matmul_mx(
+                out=acc[:],
+                lhsT=dkw_d[:, P * t : P * (t + 1)].bitcast(FP8X4),
+                lhsT_scale=dks_d[:, P * t : P * (t + 1)],
+                rhs=xqw[:].bitcast(FP8X4),
+                rhs_scale=xqs[:],
+                start=True,
+                stop=True,
+            )
+            nc.scalar.activation(a_win[t][:, :S], acc[:], ACT.Copy, scale=0.0625)
+            nc.scalar.activation(w_win[t][:, :S], acc[:], ACT.Copy, scale=ga16[:, t : t + 1])
+
+        def blend(t, start, count):
+            cols = slice(start, start + count)
+            gate = gates.tile([P, count], F32, name="gate")
+            nc.scalar.activation(gate[:], a_win[t][:].indirect(entries(n1_l, start, count)), ACT.Sigmoid)
+            nc.vector.tensor_tensor(far[:, t, cols], w_win[t][:].indirect(entries(n2_l, start, count)), gate[:], ALU.mult)
+            nc.vector.scalar_tensor_tensor(near[:, t, cols], gate[:], 1.0, w_win[t][:, cols], ALU.subtract, ALU.mult)
+
+        def weave(start, count):
+            cols = slice(start, start + count)
+            nc.vector.tensor_tensor(
+                z_view[:, start // PACK : (start + count) // PACK, :, :],
+                far[:, :, cols].rearrange("p t (c i) -> p c t i", i=PACK),
+                near[:, :, cols].rearrange("p t (c i) -> p c t i", i=PACK),
+                ALU.subtract,
+            )
+
+        for t in range(PACK - 1):
+            b_tile(t, t)
+        a_tile(0, 3)
+        blend(0, 0, S)
+        b_tile(3, 3)
+        quantise_z2()
+        for t in range(1, PACK):
+            a_tile(t, PACK + t)
+            if t < PACK - 1:
+                blend(t, 0, S)
+        for h in range(2):
+            blend(PACK - 1, HALF * h, HALF)
+            weave(HALF * h, HALF)
+
+        for t in range(PACK):
+            z_w = held("z_w%d" % t, [P, P], U32)
+            z_s = held("z_s%d" % t, [P, P], U8)
+            nc.vector.quantize_mx(out=z_w[:].bitcast(FP8X4), scales=z_s[:], in_=z_b[:, S * t : S * (t + 1)])
+            acc = psum.tile([P, S], F32, name="bank%d" % t)
+            nc.tensor.matmul_mx(
+                out=acc[:],
+                lhsT=z_w[:].bitcast(FP8X4),
+                lhsT_scale=z_s[:],
+                rhs=z2_w[:].bitcast(FP8X4),
+                rhs_scale=z2_s[:],
+                start=True,
+                stop=True,
+            )
+            if t == 0:
+                nc.scalar.activation(s_win[t][:, :S], acc[:], ACT.Copy, scale=0.0625)
+            else:
+                nc.vector.tensor_scalar(s_win[t][:, :S], acc[:], 0.0625, None, ALU.mult)
+
+        out_rows = out_0.rearrange("(p t) v -> p t v", t=PACK)
+        out_words = out_1[0].rearrange("p n t -> p (n t)").bitcast(I32)
+        o_s = held("o_s", [P, S], U8)
+        pending = []
+
+        def quantise_out(h, cols, width, o_b):
+            o_w = held("o_w%d" % h, [P, width], U32)
+            nc.vector.quantize_mx(out=o_w[:].bitcast(FP8X4), scales=o_s[:, cols], in_=o_b[:])
+            nc.sync.dma_start(out_words[:, cols], o_w[:].bitcast(I32))
+
+        start = 0
+        for h, width in enumerate(CHUNKS):
+            cols = slice(start, start + width)
+            result = held("result%d" % h, [P, PACK, width], F32)
+            joint = HALF // width
+            for t0 in range(0, PACK, joint):
+                if h == len(CHUNKS) - 1 and t0 > 0:
+                    quantise_out(*pending[0])
+                    pending.remove(pending[0])
+                members = ring.tile([P, HALF, MEMBERS], F32, name="members")
+                for j in range(joint):
+                    nc.scalar.activation(
+                        members[:, width * j : width * (j + 1), :].rearrange("p v m -> p (v m)"),
+                        s_win[t0 + j][:].indirect(entries(n5_l, MEMBERS * start, MEMBERS * width)),
+                        ACT.Copy,
+                    )
+                high = ring.tile([P, HALF, 2], F32, name="high")
+                low = ring.tile([P, HALF, 2], F32, name="low")
+                nc.vector.tensor_tensor(high[:], members[:, :, 0:2], members[:, :, 2:4], ALU.max)
+                nc.vector.tensor_tensor(low[:], members[:, :, 0:2], members[:, :, 2:4], ALU.min)
+                top = ring.tile([P, HALF], F32, name="top")
+                bottom = ring.tile([P, HALF], F32, name="bottom")
+                nc.vector.tensor_tensor(top[:], high[:, :, 0], high[:, :, 1], ALU.max)
+                nc.vector.tensor_tensor(bottom[:], low[:, :, 0], low[:, :, 1], ALU.min)
+                capped = ring.tile([P, HALF], F32, name="capped")
+                for j in range(joint):
+                    part = slice(width * j, width * (j + 1))
+                    nc.vector.scalar_tensor_tensor(capped[:, part], s_win[t0 + j][:, cols], 1.5, top[:, part], ALU.mult, ALU.min)
+                nc.vector.tensor_tensor(
+                    result[:, t0 : t0 + joint, :].rearrange("p t v -> p (t v)"), capped[:], bottom[:], ALU.max
+                )
+            nc.sync.dma_start(out_rows[:, :, cols], result[:])
+            o_b = held("o_b%d" % h, [P, width * PACK], BF16)
+            woven = o_b[:].rearrange("p (c i t) -> p c t i", i=4, t=PACK)
+            planes = result[:].rearrange("p t (c i) -> p c t i", i=4)
+            if h < len(CHUNKS) - 1:
+                nc.scalar.copy(woven, planes)
+            else:
+                nc.vector.tensor_copy(woven, planes)
+            pending.append((h, cols, width, o_b))
+            start = start + width
+        while_left = list(pending)
+        for item in while_left:
+            quantise_out(*item)
+        for q in range(4):
+            nc.sync.dma_start(out_2[0, 4 * q : 4 * q + 4, :].bitcast(I32), o_s[32 * q : 32 * q + 4, :].bitcast(I32))

@@ -51,28 +51,28 @@ def tile_picked_ckqtrackquadgclip_none_po_kernel(
         ds = held("ds", [P, G], U8)
         ww = held("ww", [P, 2 * S], U8)
         ws = held("ws", [P, S], U8)
-        nc.gpsimd.memset(ws[:].bitcast(I32), 0)
         nc.gpsimd.memset(xs[:].bitcast(I32), 0)
+        nc.vector.memset(ws[:].bitcast(I32), 0)
         nc.vector.memset(ds[:].bitcast(I32), 0)
 
         two_l = load_list("two_l", two)
         nc.sync.dma_start(xw[:].bitcast(I32), x_words[0].rearrange("p n t -> p (n t)").bitcast(I32))
-        nc.scalar.dma_start(ww[:].bitcast(I32), w1_words[0].bitcast(I32))
+        nc.gpsimd.dma_start(ww[:].bitcast(I32), w1_words[0].bitcast(I32))
+        offs_l = load_list("offs_l", offs)
         for q in range(4):
-            nc.scalar.dma_start(ws[32 * q : 32 * q + 4, :].bitcast(I32), w1_scales[0, 4 * q : 4 * q + 4, :].bitcast(I32))
-        for q, queue in enumerate((nc.gpsimd, nc.gpsimd, nc.sync, nc.sync)):
-            queue.dma_start(xs[32 * q : 32 * q + 4, :].bitcast(I32), x_scales[0, 4 * q : 4 * q + 4, :].bitcast(I32))
+            nc.sync.dma_start(xs[32 * q : 32 * q + 4, :].bitcast(I32), x_scales[0, 4 * q : 4 * q + 4, :].bitcast(I32))
+        for q in range(4):
+            nc.sync.dma_start(ws[32 * q : 32 * q + 4, :].bitcast(I32), w1_scales[0, 4 * q : 4 * q + 4, :].bitcast(I32))
+        n3_l = load_list("n3_l", n3)
         k1_l = load_list("k1_l", k1)
         for e in range(2):
             nc.sync.dma_start(ds[e:P:16, :].bitcast(I32), d_scales[0, e:16:2, :].bitcast(I32))
-        n3_l = load_list("n3_l", n3)
-        offs_l = load_list("offs_l", offs)
-        nc.sync.dma_start(dw[:].bitcast(I32), d_words[0].rearrange("p n t -> p (n t)").bitcast(I32))
         n4_l = load_list("n4_l", n4)
+        nc.sync.dma_start(dw[:].bitcast(I32), d_words[0].rearrange("p n t -> p (n t)").bitcast(I32))
         gb_raw = held("gb_raw", [P, PACK], F32)
         ga_raw = held("ga_raw", [P, PACK], F32)
-        nc.sync.dma_start(gb_raw[:], gb.rearrange("(p t) o -> p (t o)", t=PACK))
-        nc.sync.dma_start(ga_raw[:], ga.rearrange("(p t) o -> p (t o)", t=PACK))
+        nc.gpsimd.dma_start(gb_raw[:], gb.rearrange("(p t) o -> p (t o)", t=PACK))
+        nc.gpsimd.dma_start(ga_raw[:], ga.rearrange("(p t) o -> p (t o)", t=PACK))
         n1_l = load_list("n1_l", n1)
         n2_l = load_list("n2_l", n2)
         n5_l = load_list("n5_l", n5)
@@ -98,16 +98,16 @@ def tile_picked_ckqtrackquadgclip_none_po_kernel(
         x2s = held("x2s", [P, S], U8)
         nc.vector.tensor_copy(x2w[:], xw[:].indirect(two_l[:]))
         nc.vector.tensor_copy(x2s[:], xs[:].indirect(two_l[:]))
+        xqw = held("xqw", [P, S], U32)
+        xqs = held("xqs", [P, S], U8)
+        nc.vector.tensor_copy(xqw[:], xw[:].indirect(offs_l[:]))
+        nc.vector.tensor_copy(xqs[:], xs[:].indirect(offs_l[:]))
         dks = held("dks", [P, S], U8)
         dks_d = held("dks_d", [P, S], U8)
         nc.vector.tensor_copy(dks[:], ds[:].indirect(k1_l[:]))
         nc.vector.tensor_copy(dks_d[:].rearrange("p (t m) -> p t m", t=PACK), dks[:].rearrange("p (m t) -> p t m", t=PACK))
         for e in range(2):
             nc.sync.dma_start(dks_d[2 + e : P : 32, :].bitcast(I32), dks_d[16 + e : P : 32, :].bitcast(I32))
-        xqw = held("xqw", [P, S], U32)
-        xqs = held("xqs", [P, S], U8)
-        nc.vector.tensor_copy(xqw[:], xw[:].indirect(offs_l[:]))
-        nc.vector.tensor_copy(xqs[:], xs[:].indirect(offs_l[:]))
         dkw = keep.tile([P, S], U32, name="dkw", tag="first_difference", align_bytes=64)
         dkw_d = held("dkw_d", [P, S], U32)
         nc.vector.tensor_copy(dkw[:], dw[:].indirect(k1_l[:]))
@@ -117,8 +117,10 @@ def tile_picked_ckqtrackquadgclip_none_po_kernel(
         z2_w = held("z2_w", [P, S], U32)
         z2_s = held("z2_s", [P, S], U8)
 
-        def b_tile(t, bank):
-            acc = psum.tile([P, S], F32, name="bank%d" % bank)
+        d34_all = keep.tile([P, PACK, 2, S], F32, name="d34_all", tag="first_difference", align_bytes=64)
+
+        def b_tile(t):
+            acc = psum.tile([P, S], F32, name="bank%d" % t)
             nc.tensor.matmul_mx(
                 out=acc[:],
                 lhsT=ww_d[:, 2 * P * t : 2 * P * (t + 1)].bitcast(FP4X4),
@@ -128,24 +130,22 @@ def tile_picked_ckqtrackquadgclip_none_po_kernel(
                 start=True,
                 stop=True,
             )
+            if t < PACK - 1:
+                nc.scalar.copy(b_wins[t][:, :S], acc[:])
+            else:
+                nc.vector.tensor_copy(b_wins[t][:, :S], acc[:])
+
+        def b_differences(t):
             b_win = b_wins[t]
-            nc.scalar.copy(b_win[:, :S], acc[:])
             b34 = ring.tile([P, 2, S], F32, name="b34")
             for which, lst in enumerate((n3_l, n4_l)):
                 nc.scalar.activation(b34[:, which, :], b_win[:].indirect(lst[:]), ACT.Copy)
-            if t == 0:
-                d34 = keep.tile([P, 2, S], F32, name="d34_first", tag="first_difference", align_bytes=64)
-            else:
-                d34 = ring.tile([P, 2, S], F32, name="d34")
-            nc.vector.tensor_tensor(d34[:], b34[:], b_win[:, :S].unsqueeze(1).to_broadcast([P, 2, S]), ALU.subtract)
-            nc.vector.scalar_tensor_tensor(z2_planes[:, t, :], d34[:, 0, :], gb34[:, t : t + 1], d34[:, 1, :], ALU.mult, ALU.mult)
+            d34 = d34_all[:, t, :, :]
+            nc.vector.tensor_tensor(d34, b34[:], b_win[:, :S].unsqueeze(1).to_broadcast([P, 2, S]), ALU.subtract)
+            return d34
 
-        def quantise_z2():
-            z2_b = held("z2_b", [P, S * PACK], BF16)
-            nc.vector.tensor_copy(
-                z2_b[:].rearrange("p (c i t) -> p c t i", i=4, t=PACK), z2_planes[:].rearrange("p t (c i) -> p c t i", i=4)
-            )
-            nc.vector.quantize_mx(out=z2_w[:].bitcast(FP8X4), scales=z2_s[:], in_=z2_b[:])
+        def b_product(t, d34):
+            nc.vector.scalar_tensor_tensor(z2_planes[:, t, :], d34[:, 0, :], gb34[:, t : t + 1], d34[:, 1, :], ALU.mult, ALU.mult)
 
         z_b = held("z_b", [P, S * PACK], BF16)
         z_view = z_b[:].rearrange("p (i c t) -> p c t i", i=PACK, t=PACK)
@@ -164,13 +164,23 @@ def tile_picked_ckqtrackquadgclip_none_po_kernel(
                 stop=True,
             )
             nc.scalar.activation(a_win[t][:, :S], acc[:], ACT.Copy, scale=0.0625)
-            nc.scalar.activation(w_win[t][:, :S], acc[:], ACT.Copy, scale=ga16[:, t : t + 1])
+            if t < PACK // 2:
+                nc.vector.tensor_scalar(w_win[t][:, :S], a_win[t][:, :S], ga_raw[:, t : t + 1], None, ALU.mult)
+            else:
+                nc.scalar.activation(w_win[t][:, :S], acc[:], ACT.Copy, scale=ga16[:, t : t + 1])
 
-        def blend(t, start, count):
-            cols = slice(start, start + count)
+        def look_gate(t, start, count):
             gate = gates.tile([P, count], F32, name="gate")
             nc.scalar.activation(gate[:], a_win[t][:].indirect(entries(n1_l, start, count)), ACT.Sigmoid)
-            nc.vector.tensor_tensor(far[:, t, cols], w_win[t][:].indirect(entries(n2_l, start, count)), gate[:], ALU.mult)
+            return gate
+
+        def far_part(t, start, count, gate):
+            nc.vector.tensor_tensor(
+                far[:, t, start : start + count], w_win[t][:].indirect(entries(n2_l, start, count)), gate[:], ALU.mult
+            )
+
+        def near_part(t, start, count, gate):
+            cols = slice(start, start + count)
             nc.vector.scalar_tensor_tensor(near[:, t, cols], gate[:], 1.0, w_win[t][:, cols], ALU.subtract, ALU.mult)
 
         def weave(start, count):
@@ -182,19 +192,38 @@ def tile_picked_ckqtrackquadgclip_none_po_kernel(
                 ALU.subtract,
             )
 
+        b_tile(0)
+        d34_0 = b_differences(0)
+        b_tile(1)
+        d34_1 = b_differences(1)
+        b_product(0, d34_0)
+        b_tile(2)
+        b_tile(3)
+        d34_2 = b_differences(2)
+        b_product(1, d34_1)
+        b_product(2, d34_2)
+        d34_3 = b_differences(3)
+        a_tile(0, PACK)
+        b_product(3, d34_3)
         for t in range(PACK - 1):
-            b_tile(t, t)
-        a_tile(0, 3)
-        blend(0, 0, S)
-        b_tile(3, 3)
-        quantise_z2()
-        for t in range(1, PACK):
-            a_tile(t, PACK + t)
-            if t < PACK - 1:
-                blend(t, 0, S)
-        for h in range(2):
-            blend(PACK - 1, HALF * h, HALF)
-            weave(HALF * h, HALF)
+            gate = look_gate(t, 0, S)
+            far_part(t, 0, S, gate)
+            near_part(t, 0, S, gate)
+            a_tile(t + 1, PACK + t + 1)
+        last = PACK - 1
+        gate_lo = look_gate(last, 0, HALF)
+        gate_hi = look_gate(last, HALF, HALF)
+        z2_b = held("z2_b", [P, S * PACK], BF16)
+        nc.scalar.copy(
+            z2_b[:].rearrange("p (c i t) -> p c t i", i=4, t=PACK), z2_planes[:].rearrange("p t (c i) -> p c t i", i=4)
+        )
+        far_part(last, 0, HALF, gate_lo)
+        near_part(last, 0, HALF, gate_lo)
+        far_part(last, HALF, HALF, gate_hi)
+        weave(0, HALF)
+        near_part(last, HALF, HALF, gate_hi)
+        nc.vector.quantize_mx(out=z2_w[:].bitcast(FP8X4), scales=z2_s[:], in_=z2_b[:])
+        weave(HALF, HALF)
 
         for t in range(PACK):
             z_w = held("z_w%d" % t, [P, P], U32)
@@ -218,56 +247,62 @@ def tile_picked_ckqtrackquadgclip_none_po_kernel(
         out_rows = out_0.rearrange("(p t) v -> p t v", t=PACK)
         out_words = out_1[0].rearrange("p n t -> p (n t)").bitcast(I32)
         o_s = held("o_s", [P, S], U8)
-        pending = []
+        starts = [sum(CHUNKS[:h]) for h in range(len(CHUNKS))]
+        results = [held("result%d" % h, [P, PACK, width], F32) for h, width in enumerate(CHUNKS)]
+        rounded = [held("o_b%d" % h, [P, width * PACK], BF16) for h, width in enumerate(CHUNKS)]
 
-        def quantise_out(h, cols, width, o_b):
-            o_w = held("o_w%d" % h, [P, width], U32)
-            nc.vector.quantize_mx(out=o_w[:].bitcast(FP8X4), scales=o_s[:, cols], in_=o_b[:])
+        def quantise_out(h):
+            cols = slice(starts[h], starts[h] + CHUNKS[h])
+            o_w = held("o_w%d" % h, [P, CHUNKS[h]], U32)
+            nc.vector.quantize_mx(out=o_w[:].bitcast(FP8X4), scales=o_s[:, cols], in_=rounded[h][:])
             nc.sync.dma_start(out_words[:, cols], o_w[:].bitcast(I32))
 
-        start = 0
-        for h, width in enumerate(CHUNKS):
-            cols = slice(start, start + width)
-            result = held("result%d" % h, [P, PACK, width], F32)
-            joint = HALF // width
-            for t0 in range(0, PACK, joint):
-                if h == len(CHUNKS) - 1 and t0 > 0:
-                    quantise_out(*pending[0])
-                    pending.remove(pending[0])
-                members = ring.tile([P, HALF, MEMBERS], F32, name="members")
-                for j in range(joint):
-                    nc.scalar.activation(
-                        members[:, width * j : width * (j + 1), :].rearrange("p v m -> p (v m)"),
-                        s_win[t0 + j][:].indirect(entries(n5_l, MEMBERS * start, MEMBERS * width)),
-                        ACT.Copy,
-                    )
-                high = ring.tile([P, HALF, 2], F32, name="high")
-                low = ring.tile([P, HALF, 2], F32, name="low")
-                nc.vector.tensor_tensor(high[:], members[:, :, 0:2], members[:, :, 2:4], ALU.max)
-                nc.vector.tensor_tensor(low[:], members[:, :, 0:2], members[:, :, 2:4], ALU.min)
-                top = ring.tile([P, HALF], F32, name="top")
-                bottom = ring.tile([P, HALF], F32, name="bottom")
-                nc.vector.tensor_tensor(top[:], high[:, :, 0], high[:, :, 1], ALU.max)
-                nc.vector.tensor_tensor(bottom[:], low[:, :, 0], low[:, :, 1], ALU.min)
-                capped = ring.tile([P, HALF], F32, name="capped")
-                for j in range(joint):
-                    part = slice(width * j, width * (j + 1))
-                    nc.vector.scalar_tensor_tensor(capped[:, part], s_win[t0 + j][:, cols], 1.5, top[:, part], ALU.mult, ALU.min)
-                nc.vector.tensor_tensor(
-                    result[:, t0 : t0 + joint, :].rearrange("p t v -> p (t v)"), capped[:], bottom[:], ALU.max
+        def finish(h, t0, capped, bottom):
+            joint = HALF // CHUNKS[h]
+            nc.vector.tensor_tensor(
+                results[h][:, t0 : t0 + joint, :].rearrange("p t v -> p (t v)"), capped[:], bottom[:], ALU.max
+            )
+            if t0 + joint == PACK:
+                nc.sync.dma_start(out_rows[:, :, starts[h] : starts[h] + CHUNKS[h]], results[h][:])
+                woven = rounded[h][:].rearrange("p (c i t) -> p c t i", i=4, t=PACK)
+                planes = results[h][:].rearrange("p t (c i) -> p c t i", i=4)
+                if h < len(CHUNKS) - 1:
+                    nc.scalar.copy(woven, planes)
+                else:
+                    quantise_out(h - 1)
+                    nc.vector.tensor_copy(woven, planes)
+                    quantise_out(h)
+
+        units = [(h, t0) for h, width in enumerate(CHUNKS) for t0 in range(0, PACK, HALF // width)]
+        unfinished = None
+        for h, t0 in units:
+            width = CHUNKS[h]
+            cols = slice(starts[h], starts[h] + width)
+            members = ring.tile([P, HALF, MEMBERS], F32, name="members")
+            for j in range(HALF // width):
+                nc.scalar.activation(
+                    members[:, width * j : width * (j + 1), :].rearrange("p v m -> p (v m)"),
+                    s_win[t0 + j][:].indirect(entries(n5_l, MEMBERS * starts[h], MEMBERS * width)),
+                    ACT.Copy,
                 )
-            nc.sync.dma_start(out_rows[:, :, cols], result[:])
-            o_b = held("o_b%d" % h, [P, width * PACK], BF16)
-            woven = o_b[:].rearrange("p (c i t) -> p c t i", i=4, t=PACK)
-            planes = result[:].rearrange("p t (c i) -> p c t i", i=4)
-            if h < len(CHUNKS) - 1:
-                nc.scalar.copy(woven, planes)
-            else:
-                nc.vector.tensor_copy(woven, planes)
-            pending.append((h, cols, width, o_b))
-            start = start + width
-        while_left = list(pending)
-        for item in while_left:
-            quantise_out(*item)
+            high = ring.tile([P, HALF, 2], F32, name="high")
+            low = ring.tile([P, HALF, 2], F32, name="low")
+            nc.vector.tensor_tensor(high[:], members[:, :, 0:2], members[:, :, 2:4], ALU.max)
+            if unfinished is not None:
+                finish(*unfinished)
+            nc.vector.tensor_tensor(low[:], members[:, :, 0:2], members[:, :, 2:4], ALU.min)
+            top = ring.tile([P, HALF], F32, name="top")
+            bottom = ring.tile([P, HALF], F32, name="bottom")
+            nc.vector.tensor_tensor(top[:], high[:, :, 0], high[:, :, 1], ALU.max)
+            nc.vector.tensor_tensor(bottom[:], low[:, :, 0], low[:, :, 1], ALU.min)
+            capped = ring.tile([P, HALF], F32, name="capped")
+            for j in range(HALF // width):
+                part = slice(width * j, width * (j + 1))
+                nc.vector.scalar_tensor_tensor(capped[:, part], s_win[t0 + j][:, cols], 1.5, top[:, part], ALU.mult, ALU.min)
+            if (h, t0) == units[-1]:
+                quantise_out(0)
+            unfinished = (h, t0, capped, bottom)
+        finish(*unfinished)
         for q in range(4):
-            nc.sync.dma_start(out_2[0, 4 * q : 4 * q + 4, :].bitcast(I32), o_s[32 * q : 32 * q + 4, :].bitcast(I32))
+            queue = nc.scalar if q % 2 else nc.sync
+            queue.dma_start(out_2[0, 4 * q : 4 * q + 4, :].bitcast(I32), o_s[32 * q : 32 * q + 4, :].bitcast(I32))

@@ -32,6 +32,7 @@ def tile_picked_ckqtrackquadgclip_none_po_kernel(
         keep = ctx.enter_context(tc.tile_pool(name="keep", bufs=1))
         ring = ctx.enter_context(tc.tile_pool(name="ring", bufs=3))
         gates = ctx.enter_context(tc.tile_pool(name="gates", bufs=5))
+        shared = ctx.enter_context(tc.tile_pool(name="shared", bufs=1))
         psum = ctx.enter_context(tc.psum_pool(name="psum", bufs=1))
 
         def held(name, shape, dtype):
@@ -50,7 +51,7 @@ def tile_picked_ckqtrackquadgclip_none_po_kernel(
         dw = held("dw", [P, G], U32)
         ds = held("ds", [P, G], U8)
         ww = held("ww", [P, 2 * S], U8)
-        ws = held("ws", [P, S], U8)
+        ws = shared.tile([P, S], U8, name="ws", align_bytes=64, offset=512)
         nc.gpsimd.memset(xs[:].bitcast(I32), 0)
         nc.vector.memset(ws[:].bitcast(I32), 0)
         nc.vector.memset(ds[:].bitcast(I32), 0)
@@ -66,7 +67,7 @@ def tile_picked_ckqtrackquadgclip_none_po_kernel(
         n3_l = load_list("n3_l", n3)
         k1_l = load_list("k1_l", k1)
         for e in range(2):
-            nc.sync.dma_start(ds[e:P:16, :].bitcast(I32), d_scales[0, e:16:2, :].bitcast(I32))
+            nc.gpsimd.dma_start(ds[e:P:16, :].bitcast(I32), d_scales[0, e:16:2, :].bitcast(I32))
         n4_l = load_list("n4_l", n4)
         nc.sync.dma_start(dw[:].bitcast(I32), d_words[0].rearrange("p n t -> p (n t)").bitcast(I32))
         gb_raw = held("gb_raw", [P, PACK], F32)
@@ -98,8 +99,8 @@ def tile_picked_ckqtrackquadgclip_none_po_kernel(
         x2s = held("x2s", [P, S], U8)
         nc.vector.tensor_copy(x2w[:], xw[:].indirect(two_l[:]))
         nc.vector.tensor_copy(x2s[:], xs[:].indirect(two_l[:]))
-        xqw = held("xqw", [P, S], U32)
-        xqs = held("xqs", [P, S], U8)
+        xqw = shared.tile([P, S], U32, name="xqw", align_bytes=64, offset=768)
+        xqs = shared.tile([P, S], U8, name="xqs", align_bytes=64, offset=256)
         nc.vector.tensor_copy(xqw[:], xw[:].indirect(offs_l[:]))
         nc.vector.tensor_copy(xqs[:], xs[:].indirect(offs_l[:]))
         dks = held("dks", [P, S], U8)
@@ -220,10 +221,10 @@ def tile_picked_ckqtrackquadgclip_none_po_kernel(
         far_part(last, 0, HALF, gate_lo)
         near_part(last, 0, HALF, gate_lo)
         far_part(last, HALF, HALF, gate_hi)
-        weave(0, HALF)
         near_part(last, HALF, HALF, gate_hi)
-        nc.vector.quantize_mx(out=z2_w[:].bitcast(FP8X4), scales=z2_s[:], in_=z2_b[:])
+        weave(0, HALF)
         weave(HALF, HALF)
+        nc.vector.quantize_mx(out=z2_w[:].bitcast(FP8X4), scales=z2_s[:], in_=z2_b[:])
 
         for t in range(PACK):
             z_w = held("z_w%d" % t, [P, P], U32)
@@ -287,10 +288,11 @@ def tile_picked_ckqtrackquadgclip_none_po_kernel(
                 )
             high = ring.tile([P, HALF, 2], F32, name="high")
             low = ring.tile([P, HALF, 2], F32, name="low")
-            nc.vector.tensor_tensor(high[:], members[:, :, 0:2], members[:, :, 2:4], ALU.max)
+            pairs = members[:].rearrange("p v (a b) -> p (v a) b", b=2)
+            nc.vector.tensor_tensor(high[:].rearrange("p v a -> p (v a)"), pairs[:, :, 0], pairs[:, :, 1], ALU.max)
             if unfinished is not None:
                 finish(*unfinished)
-            nc.vector.tensor_tensor(low[:], members[:, :, 0:2], members[:, :, 2:4], ALU.min)
+            nc.vector.tensor_tensor(low[:].rearrange("p v a -> p (v a)"), pairs[:, :, 0], pairs[:, :, 1], ALU.min)
             top = ring.tile([P, HALF], F32, name="top")
             bottom = ring.tile([P, HALF], F32, name="bottom")
             nc.vector.tensor_tensor(top[:], high[:, :, 0], high[:, :, 1], ALU.max)

@@ -56,6 +56,10 @@ def tile_picked_ckqtrackquadgclip_none_po_kernel(
         nc.vector.memset(ws[:].bitcast(I32), 0)
         nc.vector.memset(ds[:].bitcast(I32), 0)
 
+        warm = held("warm", [P, 1], F32)
+        warm2 = held("warm2", [P, 1], F32)
+        nc.vector.memset(warm[:], 0.0)
+        nc.scalar.activation(warm2[:], warm[:], ACT.Sigmoid)
         two_l = load_list("two_l", two)
         nc.sync.dma_start(xw[:].bitcast(I32), x_words[0].rearrange("p n t -> p (n t)").bitcast(I32))
         nc.gpsimd.dma_start(ww[:].bitcast(I32), w1_words[0].bitcast(I32))

@@ -15,13 +15,25 @@ ACT = mybir.ActivationFunctionType
 
 P = 128
 PACK = 4
-T, G, S = 1024, 2048, 512
-MEMBERS = 4
+QUADRANT = 32
+GROUP = 16
+TOKENS = 1024
+CODEWORDS = 2048
+S = 512
 HALF = S // 2
-S_WINDOW = 1056
-W_WINDOW = 528
+MEMBERS = 4
+RUN = 4
+
+AB_WINDOW = 2 * S
+W_WINDOW = S + GROUP
+S_WINDOW = MEMBERS * HALF + 2 * GROUP
+
 CHUNKS = (256, 128, 128)
-FLOPS = 3 * 2 * 512 * 512 * 512
+
+B_ON_SCALAR = 2
+W_ON_VECTOR = 1
+
+FLOPS = 3 * 2 * S * S * S
 
 
 def tile_picked_ckqtrackquadgclip_none_po_kernel(
@@ -44,151 +56,167 @@ def tile_picked_ckqtrackquadgclip_none_po_kernel(
             return dst
 
         def entries(lst, start, count):
-            return lst[:, start // 16 : (start + count) // 16]
+            return lst[:, start // GROUP : (start + count) // GROUP]
 
-        xw = held("xw", [P, T], U32)
-        xs = held("xs", [P, T], U8)
-        dw = held("dw", [P, G], U32)
-        ds = held("ds", [P, G], U8)
-        ww = held("ww", [P, 2 * S], U8)
-        ws = shared.tile([P, S], U8, name="ws", align_bytes=64, offset=512)
-        nc.gpsimd.memset(xs[:].bitcast(I32), 0)
-        nc.vector.memset(ws[:].bitcast(I32), 0)
-        nc.vector.memset(ds[:].bitcast(I32), 0)
+        def scale_rows(tile, q):
+            return tile[QUADRANT * q : QUADRANT * q + PACK, :].bitcast(I32)
 
-        warm = held("warm", [P, 1], F32)
-        warm2 = held("warm2", [P, 1], F32)
-        nc.vector.memset(warm[:], 0.0)
-        nc.scalar.activation(warm2[:], warm[:], ACT.Sigmoid)
-        two_l = load_list("two_l", two)
-        nc.sync.dma_start(xw[:].bitcast(I32), x_words[0].rearrange("p n t -> p (n t)").bitcast(I32))
-        nc.gpsimd.dma_start(ww[:].bitcast(I32), w1_words[0].bitcast(I32))
-        offs_l = load_list("offs_l", offs)
-        for q in range(4):
-            nc.sync.dma_start(xs[32 * q : 32 * q + 4, :].bitcast(I32), x_scales[0, 4 * q : 4 * q + 4, :].bitcast(I32))
-        for q in range(4):
-            nc.sync.dma_start(ws[32 * q : 32 * q + 4, :].bitcast(I32), w1_scales[0, 4 * q : 4 * q + 4, :].bitcast(I32))
-        n3_l = load_list("n3_l", n3)
-        k1_l = load_list("k1_l", k1)
+        def product(bank, lhs_words, lhs_scales, rhs_words, rhs_scales):
+            acc = psum.tile([P, S], F32, name="bank%d" % bank)
+            nc.tensor.matmul_mx(
+                out=acc[:], lhsT=lhs_words, lhsT_scale=lhs_scales, rhs=rhs_words, rhs_scale=rhs_scales, start=True, stop=True
+            )
+            return acc
+
+        def weave_views(woven, rows):
+            return (
+                woven[:].rearrange("p (c i t) -> p c t i", i=RUN, t=PACK),
+                rows[:].rearrange("p t (c i) -> p c t i", i=RUN),
+            )
+
+        x_table = held("x_table", [P, TOKENS], U32)
+        x_bytes = held("x_bytes", [P, TOKENS], U8)
+        d_table = held("d_table", [P, CODEWORDS], U32)
+        d_bytes = held("d_bytes", [P, CODEWORDS], U8)
+        w1_table = held("w1_table", [P, 2 * S], U8)
+        w1_bytes = shared.tile([P, S], U8, name="w1_bytes", align_bytes=64, offset=S)
+        nc.gpsimd.memset(x_bytes[:].bitcast(I32), 0)
+        nc.vector.memset(w1_bytes[:].bitcast(I32), 0)
+        nc.vector.memset(d_bytes[:].bitcast(I32), 0)
+
+        warm_in = held("warm_in", [P, 1], F32)
+        warm_out = held("warm_out", [P, 1], F32)
+        nc.vector.memset(warm_in[:], 0.0)
+        nc.scalar.activation(warm_out[:], warm_in[:], ACT.Sigmoid)
+
+        two_list = load_list("two_list", two)
+        nc.sync.dma_start(x_table[:].bitcast(I32), x_words[0].rearrange("p n t -> p (n t)").bitcast(I32))
+        nc.gpsimd.dma_start(w1_table[:].bitcast(I32), w1_words[0].bitcast(I32))
+        offs_list = load_list("offs_list", offs)
+        for q in range(P // QUADRANT):
+            nc.sync.dma_start(scale_rows(x_bytes, q), x_scales[0, PACK * q : PACK * (q + 1), :].bitcast(I32))
+        for q in range(P // QUADRANT):
+            nc.sync.dma_start(scale_rows(w1_bytes, q), w1_scales[0, PACK * q : PACK * (q + 1), :].bitcast(I32))
+        n3_list = load_list("n3_list", n3)
+        k1_list = load_list("k1_list", k1)
         for e in range(2):
-            nc.gpsimd.dma_start(ds[e:P:16, :].bitcast(I32), d_scales[0, e:16:2, :].bitcast(I32))
-        n4_l = load_list("n4_l", n4)
-        nc.sync.dma_start(dw[:].bitcast(I32), d_words[0].rearrange("p n t -> p (n t)").bitcast(I32))
-        gb_raw = held("gb_raw", [P, PACK], F32)
-        ga_raw = held("ga_raw", [P, PACK], F32)
-        nc.gpsimd.dma_start(gb_raw[:], gb.rearrange("(p t) o -> p (t o)", t=PACK))
-        nc.gpsimd.dma_start(ga_raw[:], ga.rearrange("(p t) o -> p (t o)", t=PACK))
-        n1_l = load_list("n1_l", n1)
-        n2_l = load_list("n2_l", n2)
-        n5_l = load_list("n5_l", n5)
+            nc.gpsimd.dma_start(d_bytes[e:P:GROUP, :].bitcast(I32), d_scales[0, e::2, :].bitcast(I32))
+        n4_list = load_list("n4_list", n4)
+        nc.sync.dma_start(d_table[:].bitcast(I32), d_words[0].rearrange("p n t -> p (n t)").bitcast(I32))
+        gb_rows = held("gb_rows", [P, PACK], F32)
+        ga_rows = held("ga_rows", [P, PACK], F32)
+        nc.gpsimd.dma_start(gb_rows[:], gb.rearrange("(p t) o -> p (t o)", t=PACK))
+        nc.gpsimd.dma_start(ga_rows[:], ga.rearrange("(p t) o -> p (t o)", t=PACK))
+        n1_list = load_list("n1_list", n1)
+        n2_list = load_list("n2_list", n2)
+        n5_list = load_list("n5_list", n5)
 
-        b_wins = [held("b_win%d" % t, [P, 2 * S], F32) for t in range(PACK)]
-        a_win = [held("a_win%d" % t, [P, 2 * S], F32) for t in range(PACK)]
+        b_win = [held("b_win%d" % t, [P, AB_WINDOW], F32) for t in range(PACK)]
+        a_win = [held("a_win%d" % t, [P, AB_WINDOW], F32) for t in range(PACK)]
         w_win = [held("w_win%d" % t, [P, W_WINDOW], F32) for t in range(PACK)]
         s_win = [held("s_win%d" % t, [P, S_WINDOW], F32) for t in range(PACK)]
 
-        gb34 = held("gb34", [P, PACK], F32)
-        ga16 = held("ga16", [P, PACK], F32)
-        nc.gpsimd.tensor_scalar(ga16[:], ga_raw[:], 0.0625, 0.0, ALU.mult, ALU.add)
-        nc.gpsimd.tensor_scalar(gb34[:], gb_raw[:], 0.75, 0.0, ALU.mult, ALU.add)
+        gb_factor = held("gb_factor", [P, PACK], F32)
+        ga_factor = held("ga_factor", [P, PACK], F32)
+        nc.gpsimd.tensor_scalar(ga_factor[:], ga_rows[:], 0.0625, 0.0, ALU.mult, ALU.add)
+        nc.gpsimd.tensor_scalar(gb_factor[:], gb_rows[:], 0.75, 0.0, ALU.mult, ALU.add)
 
-        ww_d = held("ww_d", [P, 2 * S], U8)
-        ws_d = held("ws_d", [P, S], U8)
+        w1_dealt = held("w1_dealt", [P, 2 * S], U8)
+        w1_bytes_dealt = held("w1_bytes_dealt", [P, S], U8)
         nc.scalar.copy(
-            ww_d[:].bitcast(U16).rearrange("p (t m) -> p t m", t=PACK), ww[:].bitcast(U16).rearrange("p (m t) -> p t m", t=PACK)
+            w1_dealt[:].bitcast(U16).rearrange("p (t m) -> p t m", t=PACK),
+            w1_table[:].bitcast(U16).rearrange("p (m t) -> p t m", t=PACK),
         )
-        nc.vector.tensor_copy(ws_d[:].rearrange("p (t m) -> p t m", t=PACK), ws[:].rearrange("p (m t) -> p t m", t=PACK))
+        nc.vector.tensor_copy(
+            w1_bytes_dealt[:].rearrange("p (t m) -> p t m", t=PACK), w1_bytes[:].rearrange("p (m t) -> p t m", t=PACK)
+        )
 
-        x2w = held("x2w", [P, S], U32)
-        x2s = held("x2s", [P, S], U8)
-        nc.vector.tensor_copy(x2w[:], xw[:].indirect(two_l[:]))
-        nc.vector.tensor_copy(x2s[:], xs[:].indirect(two_l[:]))
-        xqw = shared.tile([P, S], U32, name="xqw", align_bytes=64, offset=768)
-        xqs = shared.tile([P, S], U8, name="xqs", align_bytes=64, offset=256)
-        nc.vector.tensor_copy(xqw[:], xw[:].indirect(offs_l[:]))
-        nc.vector.tensor_copy(xqs[:], xs[:].indirect(offs_l[:]))
-        dks = held("dks", [P, S], U8)
-        dks_d = held("dks_d", [P, S], U8)
-        nc.vector.tensor_copy(dks[:], ds[:].indirect(k1_l[:]))
-        nc.vector.tensor_copy(dks_d[:].rearrange("p (t m) -> p t m", t=PACK), dks[:].rearrange("p (m t) -> p t m", t=PACK))
+        two_words = held("two_words", [P, S], U32)
+        two_bytes = held("two_bytes", [P, S], U8)
+        nc.vector.tensor_copy(two_words[:], x_table[:].indirect(two_list[:]))
+        nc.vector.tensor_copy(two_bytes[:], x_bytes[:].indirect(two_list[:]))
+        offs_words = shared.tile([P, S], U32, name="offs_words", align_bytes=64, offset=S + HALF)
+        offs_bytes = shared.tile([P, S], U8, name="offs_bytes", align_bytes=64, offset=HALF)
+        nc.vector.tensor_copy(offs_words[:], x_table[:].indirect(offs_list[:]))
+        nc.vector.tensor_copy(offs_bytes[:], x_bytes[:].indirect(offs_list[:]))
+        k1_bytes = held("k1_bytes", [P, S], U8)
+        k1_bytes_dealt = held("k1_bytes_dealt", [P, S], U8)
+        nc.vector.tensor_copy(k1_bytes[:], d_bytes[:].indirect(k1_list[:]))
+        nc.vector.tensor_copy(
+            k1_bytes_dealt[:].rearrange("p (t m) -> p t m", t=PACK), k1_bytes[:].rearrange("p (m t) -> p t m", t=PACK)
+        )
         for e in range(2):
-            nc.sync.dma_start(dks_d[2 + e : P : 32, :].bitcast(I32), dks_d[16 + e : P : 32, :].bitcast(I32))
-        dkw = keep.tile([P, S], U32, name="dkw", tag="first_difference", align_bytes=64)
-        dkw_d = held("dkw_d", [P, S], U32)
-        nc.vector.tensor_copy(dkw[:], dw[:].indirect(k1_l[:]))
-        nc.vector.tensor_copy(dkw_d[:].rearrange("p (t m) -> p m t", t=PACK), dkw[:].rearrange("p (m t) -> p m t", t=PACK))
+            nc.sync.dma_start(
+                k1_bytes_dealt[2 + e : P : QUADRANT, :].bitcast(I32), k1_bytes_dealt[GROUP + e : P : QUADRANT, :].bitcast(I32)
+            )
+        k1_words = keep.tile([P, S], U32, name="k1_words", tag="words_then_differences", align_bytes=64)
+        k1_dealt = held("k1_dealt", [P, S], U32)
+        nc.vector.tensor_copy(k1_words[:], d_table[:].indirect(k1_list[:]))
+        nc.vector.tensor_copy(
+            k1_dealt[:].rearrange("p (t m) -> p m t", t=PACK), k1_words[:].rearrange("p (m t) -> p m t", t=PACK)
+        )
 
-        z2_planes = held("z2_planes", [P, PACK, S], BF16)
-        z2_w = held("z2_w", [P, S], U32)
-        z2_s = held("z2_s", [P, S], U8)
-
-        d34_all = keep.tile([P, PACK, 2, S], F32, name="d34_all", tag="first_difference", align_bytes=64)
+        z2_rows = held("z2_rows", [P, PACK, S], BF16)
+        z2_words = held("z2_words", [P, S], U32)
+        z2_bytes = held("z2_bytes", [P, S], U8)
+        differences = keep.tile([P, PACK, 2, S], F32, name="differences", tag="words_then_differences", align_bytes=64)
 
         def b_tile(t):
-            acc = psum.tile([P, S], F32, name="bank%d" % t)
-            nc.tensor.matmul_mx(
-                out=acc[:],
-                lhsT=ww_d[:, 2 * P * t : 2 * P * (t + 1)].bitcast(FP4X4),
-                lhsT_scale=ws_d[:, P * t : P * (t + 1)],
-                rhs=x2w[:].bitcast(FP8X4),
-                rhs_scale=x2s[:],
-                start=True,
-                stop=True,
+            acc = product(
+                t,
+                w1_dealt[:, 2 * P * t : 2 * P * (t + 1)].bitcast(FP4X4),
+                w1_bytes_dealt[:, P * t : P * (t + 1)],
+                two_words[:].bitcast(FP8X4),
+                two_bytes[:],
             )
-            if t < PACK - 1:
-                nc.scalar.copy(b_wins[t][:, :S], acc[:])
+            if t < B_ON_SCALAR:
+                nc.scalar.copy(b_win[t][:, :S], acc[:])
             else:
-                nc.vector.tensor_copy(b_wins[t][:, :S], acc[:])
+                nc.vector.tensor_copy(b_win[t][:, :S], acc[:])
 
         def b_differences(t):
-            b_win = b_wins[t]
-            b34 = ring.tile([P, 2, S], F32, name="b34")
-            for which, lst in enumerate((n3_l, n4_l)):
-                nc.scalar.activation(b34[:, which, :], b_win[:].indirect(lst[:]), ACT.Copy)
-            d34 = d34_all[:, t, :, :]
-            nc.vector.tensor_tensor(d34, b34[:], b_win[:, :S].unsqueeze(1).to_broadcast([P, 2, S]), ALU.subtract)
-            return d34
+            neighbours = ring.tile([P, 2, S], F32, name="neighbours")
+            for which, lst in enumerate((n3_list, n4_list)):
+                nc.scalar.activation(neighbours[:, which, :], b_win[t][:].indirect(lst[:]), ACT.Copy)
+            nc.vector.tensor_tensor(
+                differences[:, t, :, :], neighbours[:], b_win[t][:, :S].unsqueeze(1).to_broadcast([P, 2, S]), ALU.subtract
+            )
 
-        def b_product(t, d34):
-            nc.vector.scalar_tensor_tensor(z2_planes[:, t, :], d34[:, 0, :], gb34[:, t : t + 1], d34[:, 1, :], ALU.mult, ALU.mult)
+        def z2_tile(t):
+            nc.vector.scalar_tensor_tensor(
+                z2_rows[:, t, :], differences[:, t, 0, :], gb_factor[:, t : t + 1], differences[:, t, 1, :], ALU.mult, ALU.mult
+            )
 
-        z_b = held("z_b", [P, S * PACK], BF16)
-        z_view = z_b[:].rearrange("p (i c t) -> p c t i", i=PACK, t=PACK)
+        z_woven = held("z_woven", [P, S * PACK], BF16)
+        z_view = z_woven[:].rearrange("p (i c t) -> p c t i", i=PACK, t=PACK)
         far = held("far", [P, PACK, S], F32)
         near = held("near", [P, PACK, S], F32)
 
-        def a_tile(t, bank):
-            acc = psum.tile([P, S], F32, name="bank%d" % bank)
-            nc.tensor.matmul_mx(
-                out=acc[:],
-                lhsT=dkw_d[:, P * t : P * (t + 1)].bitcast(FP8X4),
-                lhsT_scale=dks_d[:, P * t : P * (t + 1)],
-                rhs=xqw[:].bitcast(FP8X4),
-                rhs_scale=xqs[:],
-                start=True,
-                stop=True,
+        def a_tile(t):
+            acc = product(
+                PACK + t,
+                k1_dealt[:, P * t : P * (t + 1)].bitcast(FP8X4),
+                k1_bytes_dealt[:, P * t : P * (t + 1)],
+                offs_words[:].bitcast(FP8X4),
+                offs_bytes[:],
             )
             nc.scalar.activation(a_win[t][:, :S], acc[:], ACT.Copy, scale=0.0625)
-            if t < PACK // 2:
-                nc.vector.tensor_scalar(w_win[t][:, :S], a_win[t][:, :S], ga_raw[:, t : t + 1], None, ALU.mult)
+            if t < W_ON_VECTOR:
+                nc.vector.tensor_scalar(w_win[t][:, :S], a_win[t][:, :S], ga_rows[:, t : t + 1], None, ALU.mult)
             else:
-                nc.scalar.activation(w_win[t][:, :S], acc[:], ACT.Copy, scale=ga16[:, t : t + 1])
+                nc.scalar.activation(w_win[t][:, :S], acc[:], ACT.Copy, scale=ga_factor[:, t : t + 1])
 
-        def look_gate(t, start, count):
+        def look_up_gate(t, start, count):
             gate = gates.tile([P, count], F32, name="gate")
-            nc.scalar.activation(gate[:], a_win[t][:].indirect(entries(n1_l, start, count)), ACT.Sigmoid)
+            nc.scalar.activation(gate[:], a_win[t][:].indirect(entries(n1_list, start, count)), ACT.Sigmoid)
             return gate
 
-        def far_part(t, start, count, gate):
-            nc.vector.tensor_tensor(
-                far[:, t, start : start + count], w_win[t][:].indirect(entries(n2_l, start, count)), gate[:], ALU.mult
-            )
-
-        def near_part(t, start, count, gate):
+        def blend(t, start, count, gate):
             cols = slice(start, start + count)
+            nc.vector.tensor_tensor(far[:, t, cols], w_win[t][:].indirect(entries(n2_list, start, count)), gate[:], ALU.mult)
             nc.vector.scalar_tensor_tensor(near[:, t, cols], gate[:], 1.0, w_win[t][:, cols], ALU.subtract, ALU.mult)
 
-        def weave(start, count):
+        def weave_z(start, count):
             cols = slice(start, start + count)
             nc.vector.tensor_tensor(
                 z_view[:, start // PACK : (start + count) // PACK, :, :],
@@ -197,52 +225,45 @@ def tile_picked_ckqtrackquadgclip_none_po_kernel(
                 ALU.subtract,
             )
 
-        b_tile(0)
-        d34_0 = b_differences(0)
-        b_tile(1)
-        d34_1 = b_differences(1)
-        b_product(0, d34_0)
-        b_tile(2)
-        b_tile(3)
-        d34_2 = b_differences(2)
-        b_product(1, d34_1)
-        b_product(2, d34_2)
-        d34_3 = b_differences(3)
-        a_tile(0, PACK)
-        b_product(3, d34_3)
-        for t in range(PACK - 1):
-            gate = look_gate(t, 0, S)
-            far_part(t, 0, S, gate)
-            near_part(t, 0, S, gate)
-            a_tile(t + 1, PACK + t + 1)
         last = PACK - 1
-        gate_lo = look_gate(last, 0, HALF)
-        gate_hi = look_gate(last, HALF, HALF)
-        z2_b = held("z2_b", [P, S * PACK], BF16)
-        nc.scalar.copy(
-            z2_b[:].rearrange("p (c i t) -> p c t i", i=4, t=PACK), z2_planes[:].rearrange("p t (c i) -> p c t i", i=4)
-        )
-        far_part(last, 0, HALF, gate_lo)
-        near_part(last, 0, HALF, gate_lo)
-        far_part(last, HALF, HALF, gate_hi)
-        near_part(last, HALF, HALF, gate_hi)
-        weave(0, HALF)
-        weave(HALF, HALF)
-        nc.vector.quantize_mx(out=z2_w[:].bitcast(FP8X4), scales=z2_s[:], in_=z2_b[:])
+        b_tile(0)
+        b_differences(0)
+        b_tile(1)
+        b_differences(1)
+        z2_tile(0)
+        b_tile(2)
+        b_tile(last)
+        b_differences(2)
+        z2_tile(1)
+        z2_tile(2)
+        b_differences(last)
+        a_tile(0)
+        z2_tile(last)
+        for t in range(last):
+            blend(t, 0, S, look_up_gate(t, 0, S))
+            a_tile(t + 1)
+        halves = [(start, look_up_gate(last, start, HALF)) for start in (0, HALF)]
+        z2_woven = held("z2_woven", [P, S * PACK], BF16)
+        nc.scalar.copy(*weave_views(z2_woven, z2_rows))
+        for start, gate in halves:
+            blend(last, start, HALF, gate)
+        for start in (0, HALF):
+            weave_z(start, HALF)
+        nc.vector.quantize_mx(out=z2_words[:].bitcast(FP8X4), scales=z2_bytes[:], in_=z2_woven[:])
 
+        z_words = held("z_words", [P, S], U32)
+        z_bytes = held("z_bytes", [P, S], U8)
+        for lo, hi in ((0, P), (P, S)):
+            nc.vector.quantize_mx(
+                out=z_words[:, lo:hi].bitcast(FP8X4), scales=z_bytes[:, lo:hi], in_=z_woven[:, PACK * lo : PACK * hi]
+            )
         for t in range(PACK):
-            z_w = held("z_w%d" % t, [P, P], U32)
-            z_s = held("z_s%d" % t, [P, P], U8)
-            nc.vector.quantize_mx(out=z_w[:].bitcast(FP8X4), scales=z_s[:], in_=z_b[:, S * t : S * (t + 1)])
-            acc = psum.tile([P, S], F32, name="bank%d" % t)
-            nc.tensor.matmul_mx(
-                out=acc[:],
-                lhsT=z_w[:].bitcast(FP8X4),
-                lhsT_scale=z_s[:],
-                rhs=z2_w[:].bitcast(FP8X4),
-                rhs_scale=z2_s[:],
-                start=True,
-                stop=True,
+            acc = product(
+                t,
+                z_words[:, P * t : P * (t + 1)].bitcast(FP8X4),
+                z_bytes[:, P * t : P * (t + 1)],
+                z2_words[:].bitcast(FP8X4),
+                z2_bytes[:],
             )
             if t == 0:
                 nc.scalar.activation(s_win[t][:, :S], acc[:], ACT.Copy, scale=0.0625)
@@ -251,43 +272,41 @@ def tile_picked_ckqtrackquadgclip_none_po_kernel(
 
         out_rows = out_0.rearrange("(p t) v -> p t v", t=PACK)
         out_words = out_1[0].rearrange("p n t -> p (n t)").bitcast(I32)
-        o_s = held("o_s", [P, S], U8)
+        out_bytes = held("out_bytes", [P, S], U8)
         starts = [sum(CHUNKS[:h]) for h in range(len(CHUNKS))]
         results = [held("result%d" % h, [P, PACK, width], F32) for h, width in enumerate(CHUNKS)]
-        rounded = [held("o_b%d" % h, [P, width * PACK], BF16) for h, width in enumerate(CHUNKS)]
+        rounded = [held("rounded%d" % h, [P, width * PACK], BF16) for h, width in enumerate(CHUNKS)]
 
-        def quantise_out(h):
+        def quantise_chunk(h):
             cols = slice(starts[h], starts[h] + CHUNKS[h])
-            o_w = held("o_w%d" % h, [P, CHUNKS[h]], U32)
-            nc.vector.quantize_mx(out=o_w[:].bitcast(FP8X4), scales=o_s[:, cols], in_=rounded[h][:])
-            nc.sync.dma_start(out_words[:, cols], o_w[:].bitcast(I32))
+            codes = held("codes%d" % h, [P, CHUNKS[h]], U32)
+            nc.vector.quantize_mx(out=codes[:].bitcast(FP8X4), scales=out_bytes[:, cols], in_=rounded[h][:])
+            nc.sync.dma_start(out_words[:, cols], codes[:].bitcast(I32))
 
         def finish(h, t0, capped, bottom):
-            joint = HALF // CHUNKS[h]
+            tiles = HALF // CHUNKS[h]
             nc.vector.tensor_tensor(
-                results[h][:, t0 : t0 + joint, :].rearrange("p t v -> p (t v)"), capped[:], bottom[:], ALU.max
+                results[h][:, t0 : t0 + tiles, :].rearrange("p t v -> p (t v)"), capped[:], bottom[:], ALU.max
             )
-            if t0 + joint == PACK:
+            if t0 + tiles == PACK:
                 nc.sync.dma_start(out_rows[:, :, starts[h] : starts[h] + CHUNKS[h]], results[h][:])
-                woven = rounded[h][:].rearrange("p (c i t) -> p c t i", i=4, t=PACK)
-                planes = results[h][:].rearrange("p t (c i) -> p c t i", i=4)
                 if h < len(CHUNKS) - 1:
-                    nc.scalar.copy(woven, planes)
+                    nc.scalar.copy(*weave_views(rounded[h], results[h]))
                 else:
-                    quantise_out(h - 1)
-                    nc.vector.tensor_copy(woven, planes)
-                    quantise_out(h)
+                    quantise_chunk(h - 1)
+                    nc.vector.tensor_copy(*weave_views(rounded[h], results[h]))
+                    quantise_chunk(h)
 
-        units = [(h, t0) for h, width in enumerate(CHUNKS) for t0 in range(0, PACK, HALF // width)]
+        steps = [(h, t0) for h, width in enumerate(CHUNKS) for t0 in range(0, PACK, HALF // width)]
         unfinished = None
-        for h, t0 in units:
+        for h, t0 in steps:
             width = CHUNKS[h]
             cols = slice(starts[h], starts[h] + width)
             members = ring.tile([P, HALF, MEMBERS], F32, name="members")
             for j in range(HALF // width):
                 nc.scalar.activation(
                     members[:, width * j : width * (j + 1), :].rearrange("p v m -> p (v m)"),
-                    s_win[t0 + j][:].indirect(entries(n5_l, MEMBERS * starts[h], MEMBERS * width)),
+                    s_win[t0 + j][:].indirect(entries(n5_list, MEMBERS * starts[h], MEMBERS * width)),
                     ACT.Copy,
                 )
             high = ring.tile([P, HALF, 2], F32, name="high")
@@ -305,10 +324,10 @@ def tile_picked_ckqtrackquadgclip_none_po_kernel(
             for j in range(HALF // width):
                 part = slice(width * j, width * (j + 1))
                 nc.vector.scalar_tensor_tensor(capped[:, part], s_win[t0 + j][:, cols], 1.5, top[:, part], ALU.mult, ALU.min)
-            if (h, t0) == units[-1]:
-                quantise_out(0)
+            if (h, t0) == steps[-1]:
+                quantise_chunk(0)
             unfinished = (h, t0, capped, bottom)
         finish(*unfinished)
-        for q in range(4):
+        for q in range(P // QUADRANT):
             queue = nc.scalar if q % 2 else nc.sync
-            queue.dma_start(out_2[0, 4 * q : 4 * q + 4, :].bitcast(I32), o_s[32 * q : 32 * q + 4, :].bitcast(I32))
+            queue.dma_start(out_2[0, PACK * q : PACK * (q + 1), :].bitcast(I32), scale_rows(out_bytes, q))

from contextlib import ExitStack

import concourse.mybir as mybir

F32 = mybir.dt.float32
BF16 = mybir.dt.bfloat16
I32 = mybir.dt.int32
U32 = mybir.dt.uint32
U16 = mybir.dt.uint16
U8 = mybir.dt.uint8
FP8X4 = mybir.dt.float8_e4m3fn_x4
FP4X4 = mybir.dt.float4_e2m1fn_x4
ALU = mybir.AluOpType
ACT = mybir.ActivationFunctionType

P = 128
PACK = 4
QUADRANT = 32
GROUP = 16
TOKENS = 1024
CODEWORDS = 2048
S = 512
HALF = S // 2
MEMBERS = 4
RUN = 4

AB_WINDOW = 2 * S
W_WINDOW = S + GROUP
S_WINDOW = MEMBERS * HALF + 2 * GROUP

CHUNKS = (256, 128, 128)

B_ON_SCALAR = 2
W_ON_VECTOR = 1

FLOPS = 3 * 2 * S * S * S


def tile_picked_ckqtrackquadgclip_none_po_kernel(
    tc, x_words, x_scales, d_words, d_scales, w1_words, w1_scales, ga, gb, offs, k1, two, n1, n2, n3, n4, n5, out_0, out_1, out_2
):
    nc = tc.nc
    with ExitStack() as ctx:
        keep = ctx.enter_context(tc.tile_pool(name="keep", bufs=1))
        ring = ctx.enter_context(tc.tile_pool(name="ring", bufs=3))
        gates = ctx.enter_context(tc.tile_pool(name="gates", bufs=5))
        shared = ctx.enter_context(tc.tile_pool(name="shared", bufs=1))
        psum = ctx.enter_context(tc.psum_pool(name="psum", bufs=1))

        def held(name, shape, dtype):
            return keep.tile(shape, dtype, name=name, align_bytes=64)

        def load_list(name, src):
            dst = keep.tile(list(src.shape), U16, name=name)
            nc.sync.dma_start(dst[:], src)
            return dst

        def entries(lst, start, count):
            return lst[:, start // GROUP : (start + count) // GROUP]

        def scale_rows(tile, q):
            return tile[QUADRANT * q : QUADRANT * q + PACK, :].bitcast(I32)

        def product(bank, lhs_words, lhs_scales, rhs_words, rhs_scales):
            acc = psum.tile([P, S], F32, name="bank%d" % bank)
            nc.tensor.matmul_mx(
                out=acc[:], lhsT=lhs_words, lhsT_scale=lhs_scales, rhs=rhs_words, rhs_scale=rhs_scales, start=True, stop=True
            )
            return acc

        def weave_views(woven, rows):
            return (
                woven[:].rearrange("p (c i t) -> p c t i", i=RUN, t=PACK),
                rows[:].rearrange("p t (c i) -> p c t i", i=RUN),
            )

        x_table = held("x_table", [P, TOKENS], U32)
        x_bytes = held("x_bytes", [P, TOKENS], U8)
        d_table = held("d_table", [P, CODEWORDS], U32)
        d_bytes = held("d_bytes", [P, CODEWORDS], U8)
        w1_table = held("w1_table", [P, 2 * S], U8)
        w1_bytes = shared.tile([P, S], U8, name="w1_bytes", align_bytes=64, offset=S)
        nc.gpsimd.memset(x_bytes[:].bitcast(I32), 0)
        nc.vector.memset(w1_bytes[:].bitcast(I32), 0)
        nc.vector.memset(d_bytes[:].bitcast(I32), 0)

        warm_in = held("warm_in", [P, 1], F32)
        warm_out = held("warm_out", [P, 1], F32)
        nc.vector.memset(warm_in[:], 0.0)
        nc.scalar.activation(warm_out[:], warm_in[:], ACT.Sigmoid)

        two_list = load_list("two_list", two)
        nc.sync.dma_start(x_table[:].bitcast(I32), x_words[0].rearrange("p n t -> p (n t)").bitcast(I32))
        nc.gpsimd.dma_start(w1_table[:].bitcast(I32), w1_words[0].bitcast(I32))
        offs_list = load_list("offs_list", offs)
        for q in range(P // QUADRANT):
            nc.sync.dma_start(scale_rows(x_bytes, q), x_scales[0, PACK * q : PACK * (q + 1), :].bitcast(I32))
        for q in range(P // QUADRANT):
            nc.sync.dma_start(scale_rows(w1_bytes, q), w1_scales[0, PACK * q : PACK * (q + 1), :].bitcast(I32))
        n3_list = load_list("n3_list", n3)
        k1_list = load_list("k1_list", k1)
        for e in range(2):
            nc.gpsimd.dma_start(d_bytes[e:P:GROUP, :].bitcast(I32), d_scales[0, e::2, :].bitcast(I32))
        n4_list = load_list("n4_list", n4)
        nc.sync.dma_start(d_table[:].bitcast(I32), d_words[0].rearrange("p n t -> p (n t)").bitcast(I32))
        gb_rows = held("gb_rows", [P, PACK], F32)
        ga_rows = held("ga_rows", [P, PACK], F32)
        nc.gpsimd.dma_start(gb_rows[:], gb.rearrange("(p t) o -> p (t o)", t=PACK))
        nc.gpsimd.dma_start(ga_rows[:], ga.rearrange("(p t) o -> p (t o)", t=PACK))
        n1_list = load_list("n1_list", n1)
        n2_list = load_list("n2_list", n2)
        n5_list = load_list("n5_list", n5)

        b_win = [held("b_win%d" % t, [P, AB_WINDOW], F32) for t in range(PACK)]
        a_win = [held("a_win%d" % t, [P, AB_WINDOW], F32) for t in range(PACK)]
        w_win = [held("w_win%d" % t, [P, W_WINDOW], F32) for t in range(PACK)]
        s_win = [held("s_win%d" % t, [P, S_WINDOW], F32) for t in range(PACK)]

        gb_factor = held("gb_factor", [P, PACK], F32)
        ga_factor = held("ga_factor", [P, PACK], F32)
        nc.gpsimd.tensor_scalar(ga_factor[:], ga_rows[:], 0.0625, 0.0, ALU.mult, ALU.add)
        nc.gpsimd.tensor_scalar(gb_factor[:], gb_rows[:], 0.75, 0.0, ALU.mult, ALU.add)

        w1_dealt = held("w1_dealt", [P, 2 * S], U8)
        w1_bytes_dealt = held("w1_bytes_dealt", [P, S], U8)
        nc.scalar.copy(
            w1_dealt[:].bitcast(U16).rearrange("p (t m) -> p t m", t=PACK),
            w1_table[:].bitcast(U16).rearrange("p (m t) -> p t m", t=PACK),
        )
        nc.vector.tensor_copy(
            w1_bytes_dealt[:].rearrange("p (t m) -> p t m", t=PACK), w1_bytes[:].rearrange("p (m t) -> p t m", t=PACK)
        )

        two_words = held("two_words", [P, S], U32)
        two_bytes = held("two_bytes", [P, S], U8)
        nc.vector.tensor_copy(two_words[:], x_table[:].indirect(two_list[:]))
        nc.vector.tensor_copy(two_bytes[:], x_bytes[:].indirect(two_list[:]))
        offs_words = shared.tile([P, S], U32, name="offs_words", align_bytes=64, offset=S + HALF)
        offs_bytes = shared.tile([P, S], U8, name="offs_bytes", align_bytes=64, offset=HALF)
        nc.vector.tensor_copy(offs_words[:], x_table[:].indirect(offs_list[:]))
        nc.vector.tensor_copy(offs_bytes[:], x_bytes[:].indirect(offs_list[:]))
        k1_bytes = held("k1_bytes", [P, S], U8)
        k1_bytes_dealt = held("k1_bytes_dealt", [P, S], U8)
        nc.vector.tensor_copy(k1_bytes[:], d_bytes[:].indirect(k1_list[:]))
        nc.vector.tensor_copy(
            k1_bytes_dealt[:].rearrange("p (t m) -> p t m", t=PACK), k1_bytes[:].rearrange("p (m t) -> p t m", t=PACK)
        )
        for e in range(2):
            nc.sync.dma_start(
                k1_bytes_dealt[2 + e : P : QUADRANT, :].bitcast(I32), k1_bytes_dealt[GROUP + e : P : QUADRANT, :].bitcast(I32)
            )
        k1_words = keep.tile([P, S], U32, name="k1_words", tag="words_then_differences", align_bytes=64)
        k1_dealt = held("k1_dealt", [P, S], U32)
        nc.vector.tensor_copy(k1_words[:], d_table[:].indirect(k1_list[:]))
        nc.vector.tensor_copy(
            k1_dealt[:].rearrange("p (t m) -> p m t", t=PACK), k1_words[:].rearrange("p (m t) -> p m t", t=PACK)
        )

        z2_rows = held("z2_rows", [P, PACK, S], BF16)
        z2_words = held("z2_words", [P, S], U32)
        z2_bytes = held("z2_bytes", [P, S], U8)
        differences = keep.tile([P, PACK, 2, S], F32, name="differences", tag="words_then_differences", align_bytes=64)

        def b_tile(t):
            acc = product(
                t,
                w1_dealt[:, 2 * P * t : 2 * P * (t + 1)].bitcast(FP4X4),
                w1_bytes_dealt[:, P * t : P * (t + 1)],
                two_words[:].bitcast(FP8X4),
                two_bytes[:],
            )
            if t < B_ON_SCALAR:
                nc.scalar.copy(b_win[t][:, :S], acc[:])
            else:
                nc.vector.tensor_copy(b_win[t][:, :S], acc[:])

        def b_differences(t):
            neighbours = ring.tile([P, 2, S], F32, name="neighbours")
            for which, lst in enumerate((n3_list, n4_list)):
                nc.scalar.activation(neighbours[:, which, :], b_win[t][:].indirect(lst[:]), ACT.Copy)
            nc.vector.tensor_tensor(
                differences[:, t, :, :], neighbours[:], b_win[t][:, :S].unsqueeze(1).to_broadcast([P, 2, S]), ALU.subtract
            )

        def z2_tile(t):
            nc.vector.scalar_tensor_tensor(
                z2_rows[:, t, :], differences[:, t, 0, :], gb_factor[:, t : t + 1], differences[:, t, 1, :], ALU.mult, ALU.mult
            )

        z_woven = held("z_woven", [P, S * PACK], BF16)
        z_view = z_woven[:].rearrange("p (i c t) -> p c t i", i=PACK, t=PACK)
        far = held("far", [P, PACK, S], F32)
        near = held("near", [P, PACK, S], F32)

        def a_tile(t):
            acc = product(
                PACK + t,
                k1_dealt[:, P * t : P * (t + 1)].bitcast(FP8X4),
                k1_bytes_dealt[:, P * t : P * (t + 1)],
                offs_words[:].bitcast(FP8X4),
                offs_bytes[:],
            )
            nc.scalar.activation(a_win[t][:, :S], acc[:], ACT.Copy, scale=0.0625)
            if t < W_ON_VECTOR:
                nc.vector.tensor_scalar(w_win[t][:, :S], a_win[t][:, :S], ga_rows[:, t : t + 1], None, ALU.mult)
            else:
                nc.scalar.activation(w_win[t][:, :S], acc[:], ACT.Copy, scale=ga_factor[:, t : t + 1])

        def look_up_gate(t, start, count):
            gate = gates.tile([P, count], F32, name="gate")
            nc.scalar.activation(gate[:], a_win[t][:].indirect(entries(n1_list, start, count)), ACT.Sigmoid)
            return gate

        def blend(t, start, count, gate):
            cols = slice(start, start + count)
            nc.vector.tensor_tensor(far[:, t, cols], w_win[t][:].indirect(entries(n2_list, start, count)), gate[:], ALU.mult)
            nc.vector.scalar_tensor_tensor(near[:, t, cols], gate[:], 1.0, w_win[t][:, cols], ALU.subtract, ALU.mult)

        def weave_z(start, count):
            cols = slice(start, start + count)
            nc.vector.tensor_tensor(
                z_view[:, start // PACK : (start + count) // PACK, :, :],
                far[:, :, cols].rearrange("p t (c i) -> p c t i", i=PACK),
                near[:, :, cols].rearrange("p t (c i) -> p c t i", i=PACK),
                ALU.subtract,
            )

        last = PACK - 1
        b_tile(0)
        b_differences(0)
        b_tile(1)
        b_differences(1)
        z2_tile(0)
        b_tile(2)
        b_tile(last)
        b_differences(2)
        z2_tile(1)
        z2_tile(2)
        b_differences(last)
        a_tile(0)
        z2_tile(last)
        for t in range(last):
            blend(t, 0, S, look_up_gate(t, 0, S))
            a_tile(t + 1)
        halves = [(start, look_up_gate(last, start, HALF)) for start in (0, HALF)]
        z2_woven = held("z2_woven", [P, S * PACK], BF16)
        nc.scalar.copy(*weave_views(z2_woven, z2_rows))
        for start, gate in halves:
            blend(last, start, HALF, gate)
        for start in (0, HALF):
            weave_z(start, HALF)
        nc.vector.quantize_mx(out=z2_words[:].bitcast(FP8X4), scales=z2_bytes[:], in_=z2_woven[:])

        z_words = held("z_words", [P, S], U32)
        z_bytes = held("z_bytes", [P, S], U8)
        for lo, hi in ((0, P), (P, S)):
            nc.vector.quantize_mx(
                out=z_words[:, lo:hi].bitcast(FP8X4), scales=z_bytes[:, lo:hi], in_=z_woven[:, PACK * lo : PACK * hi]
            )
        for t in range(PACK):
            acc = product(
                t,
                z_words[:, P * t : P * (t + 1)].bitcast(FP8X4),
                z_bytes[:, P * t : P * (t + 1)],
                z2_words[:].bitcast(FP8X4),
                z2_bytes[:],
            )
            if t == 0:
                nc.scalar.activation(s_win[t][:, :S], acc[:], ACT.Copy, scale=0.0625)
            else:
                nc.vector.tensor_scalar(s_win[t][:, :S], acc[:], 0.0625, None, ALU.mult)

        out_rows = out_0.rearrange("(p t) v -> p t v", t=PACK)
        out_words = out_1[0].rearrange("p n t -> p (n t)").bitcast(I32)
        out_bytes = held("out_bytes", [P, S], U8)
        starts = [sum(CHUNKS[:h]) for h in range(len(CHUNKS))]
        results = [held("result%d" % h, [P, PACK, width], F32) for h, width in enumerate(CHUNKS)]
        rounded = [held("rounded%d" % h, [P, width * PACK], BF16) for h, width in enumerate(CHUNKS)]

        def quantise_chunk(h):
            cols = slice(starts[h], starts[h] + CHUNKS[h])
            codes = held("codes%d" % h, [P, CHUNKS[h]], U32)
            nc.vector.quantize_mx(out=codes[:].bitcast(FP8X4), scales=out_bytes[:, cols], in_=rounded[h][:])
            nc.sync.dma_start(out_words[:, cols], codes[:].bitcast(I32))

        def finish(h, t0, capped, bottom):
            tiles = HALF // CHUNKS[h]
            nc.vector.tensor_tensor(
                results[h][:, t0 : t0 + tiles, :].rearrange("p t v -> p (t v)"), capped[:], bottom[:], ALU.max
            )
            if t0 + tiles == PACK:
                nc.sync.dma_start(out_rows[:, :, starts[h] : starts[h] + CHUNKS[h]], results[h][:])
                if h < len(CHUNKS) - 1:
                    nc.scalar.copy(*weave_views(rounded[h], results[h]))
                else:
                    quantise_chunk(h - 1)
                    nc.vector.tensor_copy(*weave_views(rounded[h], results[h]))
                    quantise_chunk(h)

        steps = [(h, t0) for h, width in enumerate(CHUNKS) for t0 in range(0, PACK, HALF // width)]
        unfinished = None
        for h, t0 in steps:
            width = CHUNKS[h]
            cols = slice(starts[h], starts[h] + width)
            members = ring.tile([P, HALF, MEMBERS], F32, name="members")
            for j in range(HALF // width):
                nc.scalar.activation(
                    members[:, width * j : width * (j + 1), :].rearrange("p v m -> p (v m)"),
                    s_win[t0 + j][:].indirect(entries(n5_list, MEMBERS * starts[h], MEMBERS * width)),
                    ACT.Copy,
                )
            high = ring.tile([P, HALF, 2], F32, name="high")
            low = ring.tile([P, HALF, 2], F32, name="low")
            pairs = members[:].rearrange("p v (a b) -> p (v a) b", b=2)
            nc.vector.tensor_tensor(high[:].rearrange("p v a -> p (v a)"), pairs[:, :, 0], pairs[:, :, 1], ALU.max)
            if unfinished is not None:
                finish(*unfinished)
            nc.vector.tensor_tensor(low[:].rearrange("p v a -> p (v a)"), pairs[:, :, 0], pairs[:, :, 1], ALU.min)
            top = ring.tile([P, HALF], F32, name="top")
            bottom = ring.tile([P, HALF], F32, name="bottom")
            nc.vector.tensor_tensor(top[:], high[:, :, 0], high[:, :, 1], ALU.max)
            nc.vector.tensor_tensor(bottom[:], low[:, :, 0], low[:, :, 1], ALU.min)
            capped = ring.tile([P, HALF], F32, name="capped")
            for j in range(HALF // width):
                part = slice(width * j, width * (j + 1))
                nc.vector.scalar_tensor_tensor(capped[:, part], s_win[t0 + j][:, cols], 1.5, top[:, part], ALU.mult, ALU.min)
            if (h, t0) == steps[-1]:
                quantise_chunk(0)
            unfinished = (h, t0, capped, bottom)
        finish(*unfinished)
        for q in range(P // QUADRANT):
            queue = nc.scalar if q % 2 else nc.sync
            queue.dma_start(out_2[0, PACK * q : PACK * (q + 1), :].bitcast(I32), scale_rows(out_bytes, q))
